import numpy as np
import ml_dtypes


def mxq(x, axis, fmt="e4m3"):
    dtype, down = {"e4m3": (ml_dtypes.float8_e4m3fn, 7), "e5m2": (ml_dtypes.float8_e5m2, 14)}[fmt]
    v = np.moveaxis(np.asarray(x, np.float32).astype(ml_dtypes.bfloat16).astype(np.float64), axis, -1)
    blocks = v.reshape(v.shape[:-1] + (-1, 32))
    amax = np.abs(blocks).max(-1, keepdims=True)
    byte = np.maximum(np.where(amax > 0, np.frexp(amax)[1] - 1 + 127, 0) - down, 1)
    scale = np.exp2(byte - 127.0)
    codes = (blocks / scale).astype(np.float32).astype(dtype).astype(np.float64)
    return np.moveaxis((codes * scale).reshape(v.shape), -1, axis)


WIDE = False


def mx_kscale(k):
    if not WIDE:
        return np.ones(k)
    levels = np.array([10, -10, 5, -5, 0])
    if k % 512:
        return np.exp2(np.random.permutation(np.resize(levels, k // 32))).repeat(32)
    a = np.empty((k // 512, 16))
    for p in range(k // 512):
        a[p, :8] = np.random.permutation(np.resize(levels, 8))
        for g in range(8):
            far = levels[np.abs(levels - a[p, g]) >= 10]
            a[p, g + 8] = far[np.random.randint(len(far))]
    return np.exp2(a.ravel()).repeat(32)


def f64(x):
    return np.asarray(x).astype(np.float64)


def striped(idx):
    return np.tile(np.asarray(idx).reshape(-1, 16).T, (8, 1)).astype(np.uint16)


def unstriped(offs):
    return offs[:16].T.reshape(-1).astype(np.int64)


E2M1 = np.array([0.0, 0.5, 1.0, 1.5, 2.0, 3.0, 4.0, 6.0, -0.0, -0.5, -1.0, -1.5, -2.0, -3.0, -4.0, -6.0])


def pack_weight(w, fmt):
    k, n = w.shape
    w = f64(np.asarray(w, np.float32).astype(ml_dtypes.bfloat16)).reshape(k // 32, 32, n)
    amax = np.abs(w).max(1)
    if fmt == "e4m3":
        byte = np.frexp(amax)[1] - 1 + 127 - 7
    else:
        mant, ex = np.frexp(amax / 6.0)
        byte = np.where(mant > 0.5, ex, ex - 1) + 127
    byte = np.clip(np.where(amax > 0, byte, 1), 1, 254)
    scaled = (w * np.exp2(127.0 - byte)[:, None, :]).reshape(k, n).astype(np.float32)
    by_word = np.ascontiguousarray(scaled.reshape(k // 512, 128, 4, n).transpose(0, 1, 3, 2))
    if fmt == "e4m3":
        words = by_word.astype(ml_dtypes.float8_e4m3fn).view(np.uint8)
    else:
        c = by_word.astype(ml_dtypes.float4_e2m1fn).view(np.uint8) & 0xF
        words = (c[..., 0::2] | (c[..., 1::2] << 4)).reshape(k // 512, 128, 2 * n)
    return np.ascontiguousarray(words), np.ascontiguousarray(byte.astype(np.uint8).reshape(k // 512, 16, n))


def unpack_weight(words, scales, fmt):
    g, _, n = scales.shape
    words = np.ascontiguousarray(words).reshape(g, 128, n, -1)
    if fmt == "e4m3":
        vals = words.view(ml_dtypes.float8_e4m3fn).astype(np.float64)
    else:
        nib = np.empty((g, 128, n, 4), np.uint8)
        nib[..., 0::2] = words & 0xF
        nib[..., 1::2] = words >> 4
        vals = E2M1[nib]
    vals = vals * np.repeat(np.exp2(scales.astype(np.float64) - 127.0), 8, axis=1)[..., None]
    return vals.transpose(0, 1, 3, 2).reshape(g * 512, n)


def e4m3fn_bytes(y):
    return np.clip(np.asarray(y, np.float64), -448.0, 448.0).astype(np.float32).astype(ml_dtypes.float8_e4m3fn).view(np.uint8)


def e4m3fn_values(b):
    return np.asarray(b, np.uint8).view(ml_dtypes.float8_e4m3fn).astype(np.float64)


K, T, V, J, R, N = 512, 1024, 2048, 256, 512, 256


def setup_inputs():
    n = np.random.standard_normal
    idx = np.random.permutation(V)[:R]
    idx2 = np.random.permutation(V)[:R]
    idx3 = np.random.permutation(T)[:J]
    fk = mx_kscale(K)
    fr = mx_kscale(R)
    xtp = pack_weight(n((K, T)) / fk[:, None], "e2m1")
    wbp = pack_weight(n((R, N)) * 1 / np.sqrt(R) / fr[:, None], "e4m3")
    return {
        "xt_words": xtp[0],
        "xt_scales": xtp[1],
        "ca": e4m3fn_bytes(60.0 * n((K, V))),
        "sa": (np.random.uniform(0.0004, 0.0012, (K, 1)) * fk[:, None]).astype(np.float32),
        "sb": (np.random.uniform(0.0004, 0.0012, (K, 1)) * fk[:, None]).astype(np.float32),
        "sr": (np.random.uniform(0.5, 1.6, (R, 1)) * fr[:, None]).astype(np.float32),
        "wb_words": wbp[0],
        "wb_scales": wbp[1],
        "offs": striped(idx),
        "offs2": striped(idx2),
        "offs3": striped(idx3),
    }


def reference(xt_words, xt_scales, ca, sa, sb, sr, wb_words, wb_scales, offs, offs2, offs3):
    idx = unstriped(offs)
    idx2 = unstriped(offs2)
    idx3 = unstriped(offs3)
    xtu = unpack_weight(xt_words, xt_scales, "e2m1")
    wbu = unpack_weight(wb_words, wb_scales, "e4m3")
    wa = e4m3fn_values(ca)[:, idx] * f64(sa)
    wc = e4m3fn_values(ca)[:, idx2] * f64(sb)
    waq = mxq(wa, 0, "e4m3")
    xtidx3g = xtu[:, idx3]
    a = waq.T @ xtidx3g
    wcq = mxq(wc, 0, "e4m3")
    b = wcq.T @ xtidx3g
    hid = np.maximum(a, b) * f64(sr)
    hidq = mxq(hid, 0, "e4m3")
    p = wbu.T @ hidq
    return p

@@ -1,0 +1,188 @@
+from contextlib import ExitStack
+
+import concourse.mybir as mybir
+
+K, T, V, J, R, N = 512, 1024, 2048, 256, 512, 256
+FLOPS = 2 * (2 * K * R * J + R * N * J)
+
+F32 = mybir.dt.float32
+BF16 = mybir.dt.bfloat16
+I32 = mybir.dt.int32
+U16 = mybir.dt.uint16
+U8 = mybir.dt.uint8
+FP8 = mybir.dt.float8_e4m3fn
+FP8X4 = mybir.dt.float8_e4m3fn_x4
+FP4X4 = mybir.dt.float4_e2m1fn_x4
+COPY = mybir.ActivationFunctionType.Copy
+MAX = mybir.AluOpType.max
+MULT = mybir.AluOpType.mult
+
+P = 128
+PACK = 4
+HALVES = 2
+HALF = R // HALVES
+HALF_M = HALF // PACK
+J_PARTS = 2
+J_PART = J // J_PARTS
+VECTOR_T = 3
+
+
+def tile_list_rivalcolumns_kernel(tc, xt_words, xt_scales, ca, sa, sb, sr, wb_words, wb_scales, offs, offs2, offs3, out):
+    nc = tc.nc
+    with ExitStack() as ctx:
+        pool = ctx.enter_context(tc.tile_pool(name="pool", bufs=1))
+        psum = ctx.enter_context(tc.psum_pool(name="psum", bufs=1))
+
+        list_a = pool.tile([P, R // 16], U16, name="list_a")
+        list_b = pool.tile([P, R // 16], U16, name="list_b")
+        list_x = pool.tile([P, J // 16], U16, name="list_x")
+        table = [pool.tile([P, V], U8, name="table%d" % i) for i in range(PACK)]
+        step_a = pool.tile([P, PACK], F32, name="step_a")
+        step_b = pool.tile([P, PACK], F32, name="step_b")
+        weight_r = pool.tile([P, PACK], F32, name="weight_r")
+        x_words = pool.tile([P, T], U16, name="x_words")
+        x_scales = pool.tile([P, T], U8, name="x_scales")
+        wb_codes = pool.tile([P, N], I32, name="wb_codes", align_bytes=64)
+        wb_plane = pool.tile([P, N], U8, name="wb_plane", align_bytes=64)
+
+        nc.vector.memset(x_scales[:].bitcast(I32), 0)
+        nc.vector.memset(wb_plane[:].bitcast(I32), 0)
+
+        ca_rows = ca.rearrange("(p i) v -> p i v", i=PACK)
+        nc.sync.dma_start(list_a[:], offs)
+        nc.scalar.dma_start(step_a[:], sa.rearrange("(p i) o -> p (i o)", i=PACK))
+        for i in range(PACK):
+            nc.sync.dma_start(table[i][:], ca_rows[:, i, :])
+        nc.sync.dma_start(list_x[:], offs3)
+        nc.sync.dma_start(x_words[:].bitcast(I32), xt_words[0].bitcast(I32))
+        for q in range(4):
+            nc.sync.dma_start(x_scales[32 * q : 32 * q + 4, :].bitcast(I32), xt_scales[0, 4 * q : 4 * q + 4, :].bitcast(I32))
+        nc.sync.dma_start(list_b[:], offs2)
+        nc.sync.dma_start(step_b[:], sb.rearrange("(p i) o -> p (i o)", i=PACK))
+        nc.sync.dma_start(weight_r[:], sr.rearrange("(p t) o -> p (t o)", t=PACK))
+        nc.sync.dma_start(wb_codes[:], wb_words[0].rearrange("p n t -> p (n t)").bitcast(I32))
+        for q in range(4):
+            nc.sync.dma_start(wb_plane[32 * q : 32 * q + 4, :].bitcast(I32), wb_scales[0, 4 * q : 4 * q + 4, :].bitcast(I32))
+
+        def look_up(name, offsets, step, half, picked):
+            planes = pool.tile([P, PACK, HALF], BF16, name="planes_" + name)
+            cols = HALF // 16
+            for i in range(PACK):
+                nc.vector.tensor_copy(picked[i], table[i][:].indirect(offsets[:, half * cols : (half + 1) * cols]))
+                nc.scalar.activation(out=planes[:, i, :], in_=picked[i].bitcast(FP8), func=COPY, scale=step[:, i : i + 1])
+            return planes
+
+        def picked_tile(name, count, tag):
+            picked = pool.tile([P, count, HALF], U8, name=name, tag=tag, align_bytes=64)
+            return [picked[:, i, :] for i in range(count)]
+
+        def weave(copy, woven, planes, t0, t1):
+            copy(
+                woven[:, t0:t1, :, :].rearrange("p t m i -> p m i t"),
+                planes[:].rearrange("p i (m t) -> p m i t", t=PACK)[:, :, :, t0:t1],
+            )
+
+        woven_a = pool.tile([P, PACK, P, PACK], BF16, name="woven_a", tag="woven_a", align_bytes=64)
+        woven_b = [pool.tile([P, PACK, HALF_M, PACK], BF16, name="woven_b%d" % h, align_bytes=64) for h in range(HALVES)]
+        picked = picked_tile("picked_a0_01", 2, "a0_01") + picked_tile("picked_a0_2", 1, "a0_2") + picked_tile("picked_a0_3", 1, "a0_3")
+        planes = look_up("a0", list_a, step_a, 0, picked)
+        weave(nc.scalar.copy, woven_a[:, :, :HALF_M, :], planes, 0, PACK)
+        planes = look_up("a1", list_a, step_a, 1, picked_tile("picked_a1", 4, "a0_2"))
+        weave(nc.scalar.copy, woven_a[:, :, HALF_M:, :], planes, 0, PACK)
+
+        xg_words = pool.tile([P, J], U16, name="xg_words", align_bytes=64)
+        xg_scales = pool.tile([P, J], U8, name="xg_scales", align_bytes=64)
+        nc.vector.tensor_copy(xg_words[:], x_words[:].indirect(list_x[:]))
+        nc.vector.tensor_copy(xg_scales[:], x_scales[:].indirect(list_x[:]))
+
+        a_codes = pool.tile([P, R], I32, name="a_codes", align_bytes=64)
+        a_plane = pool.tile([P, R], U8, name="a_plane", align_bytes=64)
+        nc.vector.quantize_mx(out=a_codes[:].bitcast(FP8X4), scales=a_plane[:], in_=woven_a[:].rearrange("p t m i -> p (t m i)"))
+
+        planes = look_up("b0", list_b, step_b, 0, picked_tile("picked_b0", 4, "b0"))
+        weave(nc.scalar.copy, woven_b[0][:], planes, 0, PACK)
+        planes = look_up("b1", list_b, step_b, 1, picked_tile("picked_b1_01", 2, "b1_01") + picked_tile("picked_b1_23", 2, "woven_a"))
+
+        b_codes = [pool.tile([P, P], I32, name="b_codes%d" % t, align_bytes=64) for t in range(PACK)]
+        b_plane = [pool.tile([P, P], U8, name="b_plane%d" % t, align_bytes=64) for t in range(PACK)]
+
+        def quantize_b(t, half):
+            cols = slice(half * HALF_M, (half + 1) * HALF_M)
+            nc.vector.quantize_mx(
+                out=b_codes[t][:, cols].bitcast(FP8X4),
+                scales=b_plane[t][:, cols],
+                in_=woven_b[half][:, t, :, :].rearrange("p m i -> p (m i)"),
+            )
+
+        for t in range(PACK):
+            quantize_b(t, 0)
+        weave(nc.scalar.copy, woven_b[1][:], planes, VECTOR_T, PACK)
+        weave(nc.vector.tensor_copy, woven_b[1][:], planes, 0, VECTOR_T)
+
+        def first_product(acc, codes, plane):
+            nc.tensor.matmul_mx(
+                out=acc,
+                lhsT=codes.bitcast(FP8X4),
+                lhsT_scale=plane,
+                rhs=xg_words[:].bitcast(FP4X4),
+                rhs_scale=xg_scales[:],
+                start=True,
+                stop=True,
+            )
+
+        a_kept = []
+        for u in range(2):
+            a_bank = psum.tile([P, 2, J], F32, name="a_bank%d" % u)
+            for e in range(2):
+                cols = slice((2 * u + e) * P, (2 * u + e + 1) * P)
+                first_product(a_bank[:, e, :], a_codes[:, cols], a_plane[:, cols])
+            kept = pool.tile([P, J, 2], F32, name="a_kept%d" % u)
+            nc.scalar.copy(kept[:], a_bank[:].rearrange("p e j -> p j e"))
+            a_kept.append(kept)
+
+        b_banks = []
+        for u in range(2):
+            b_bank = psum.tile([P, 2, J], F32, name="b_bank%d" % u)
+            for e in range(2):
+                t = 2 * u + e
+                quantize_b(t, 1)
+                first_product(b_bank[:, e, :], b_codes[t][:], b_plane[t][:])
+            b_banks.append(b_bank)
+
+        larger = pool.tile([P, 2, J, 2], F32, name="larger")
+        for u in range(2):
+            nc.vector.tensor_tensor(larger[:, u, :, :], b_banks[u][:].rearrange("p e j -> p j e"), a_kept[u][:], MAX)
+
+        hids = []
+        for c in range(J_PARTS):
+            hid = pool.tile([P, J_PART, 2, 2], BF16, name="hid%d" % c, align_bytes=64)
+            nc.vector.tensor_tensor(
+                hid[:],
+                larger[:, :, c * J_PART : (c + 1) * J_PART, :].rearrange("p u j e -> p j u e"),
+                weight_r[:].rearrange("p (u e) -> p u e", u=2).unsqueeze(1).to_broadcast([P, J_PART, 2, 2]),
+                MULT,
+            )
+            hids.append(hid)
+
+        out_rows = out.rearrange("(g p) j -> p g j", p=P)
+        for c in range(J_PARTS):
+            h_codes = pool.tile([P, J_PART], I32, name="h_codes%d" % c, align_bytes=64)
+            h_plane = pool.tile([P, J_PART], U8, name="h_plane%d" % c, align_bytes=64)
+            nc.vector.quantize_mx(out=h_codes[:].bitcast(FP8X4), scales=h_plane[:], in_=hids[c][:].rearrange("p j u e -> p (j u e)"))
+            o_bank = psum.tile([P, N // P, J_PART], F32, name="o_bank%d" % c)
+            for g in range(N // P):
+                nc.tensor.matmul_mx(
+                    out=o_bank[:, g, :],
+                    lhsT=wb_codes[:, g * P : (g + 1) * P].bitcast(FP8X4),
+                    lhsT_scale=wb_plane[:, g * P : (g + 1) * P],
+                    rhs=h_codes[:].bitcast(FP8X4),
+                    rhs_scale=h_plane[:],
+                    start=True,
+                    stop=True,
+                )
+            result = pool.tile([P, N // P, J_PART], F32, name="result%d" % c)
+            if c == 0:
+                nc.scalar.copy(result[:], o_bank[:])
+            else:
+                nc.vector.tensor_copy(result[:], o_bank[:])
+            nc.sync.dma_start(out_rows[:, :, c * J_PART : (c + 1) * J_PART], result[:])

@@ -24,7 +24,7 @@ HALF = R // HALVES
 HALF_M = HALF // PACK
 J_PARTS = 2
 J_PART = J // J_PARTS
-VECTOR_T = 3
+VECTOR_T = 2
 
 
 def tile_list_rivalcolumns_kernel(tc, xt_words, xt_scales, ca, sa, sb, sr, wb_words, wb_scales, offs, offs2, offs3, out):
@@ -49,23 +49,24 @@ def tile_list_rivalcolumns_kernel(tc, xt_words, xt_scales, ca, sa, sb, sr, wb_wo
         nc.vector.memset(wb_plane[:].bitcast(I32), 0)
 
         ca_rows = ca.rearrange("(p i) v -> p i v", i=PACK)
+        nc.sync.dma_start(table[0][:], ca_rows[:, 0, :])
         nc.sync.dma_start(list_a[:], offs)
         nc.scalar.dma_start(step_a[:], sa.rearrange("(p i) o -> p (i o)", i=PACK))
-        for i in range(PACK):
+        for i in range(1, PACK):
             nc.sync.dma_start(table[i][:], ca_rows[:, i, :])
+        nc.sync.dma_start(list_b[:], offs2)
+        nc.sync.dma_start(step_b[:], sb.rearrange("(p i) o -> p (i o)", i=PACK))
         nc.sync.dma_start(list_x[:], offs3)
         nc.sync.dma_start(x_words[:].bitcast(I32), xt_words[0].bitcast(I32))
         for q in range(4):
             nc.sync.dma_start(x_scales[32 * q : 32 * q + 4, :].bitcast(I32), xt_scales[0, 4 * q : 4 * q + 4, :].bitcast(I32))
-        nc.sync.dma_start(list_b[:], offs2)
-        nc.sync.dma_start(step_b[:], sb.rearrange("(p i) o -> p (i o)", i=PACK))
         nc.sync.dma_start(weight_r[:], sr.rearrange("(p t) o -> p (t o)", t=PACK))
         nc.sync.dma_start(wb_codes[:], wb_words[0].rearrange("p n t -> p (n t)").bitcast(I32))
         for q in range(4):
             nc.sync.dma_start(wb_plane[32 * q : 32 * q + 4, :].bitcast(I32), wb_scales[0, 4 * q : 4 * q + 4, :].bitcast(I32))
 
         def look_up(name, offsets, step, half, picked):
-            planes = pool.tile([P, PACK, HALF], BF16, name="planes_" + name)
+            planes = pool.tile([P, PACK, HALF], BF16, name="planes_" + name, tag="planes")
             cols = HALF // 16
             for i in range(PACK):
                 nc.vector.tensor_copy(picked[i], table[i][:].indirect(offsets[:, half * cols : (half + 1) * cols]))
@@ -82,97 +83,114 @@ def tile_list_rivalcolumns_kernel(tc, xt_words, xt_scales, ca, sa, sb, sr, wb_wo
                 planes[:].rearrange("p i (m t) -> p m i t", t=PACK)[:, :, :, t0:t1],
             )
 
-        woven_a = pool.tile([P, PACK, P, PACK], BF16, name="woven_a", tag="woven_a", align_bytes=64)
-        woven_b = [pool.tile([P, PACK, HALF_M, PACK], BF16, name="woven_b%d" % h, align_bytes=64) for h in range(HALVES)]
+        woven_a = pool.tile([P, PACK, P, PACK], BF16, name="woven_a", align_bytes=64)
         picked = picked_tile("picked_a0_01", 2, "a0_01") + picked_tile("picked_a0_2", 1, "a0_2") + picked_tile("picked_a0_3", 1, "a0_3")
         planes = look_up("a0", list_a, step_a, 0, picked)
         weave(nc.scalar.copy, woven_a[:, :, :HALF_M, :], planes, 0, PACK)
         planes = look_up("a1", list_a, step_a, 1, picked_tile("picked_a1", 4, "a0_2"))
         weave(nc.scalar.copy, woven_a[:, :, HALF_M:, :], planes, 0, PACK)
 
+        woven_b = pool.tile([P, PACK, P, PACK], BF16, name="woven_b", align_bytes=64)
+        planes = look_up("b0", list_b, step_b, 0, picked_tile("picked_b0", 4, "a0_3"))
+        weave(nc.scalar.copy, woven_b[:, :, :HALF_M, :], planes, 0, PACK)
+
         xg_words = pool.tile([P, J], U16, name="xg_words", align_bytes=64)
         xg_scales = pool.tile([P, J], U8, name="xg_scales", align_bytes=64)
         nc.vector.tensor_copy(xg_words[:], x_words[:].indirect(list_x[:]))
         nc.vector.tensor_copy(xg_scales[:], x_scales[:].indirect(list_x[:]))
 
-        a_codes = pool.tile([P, R], I32, name="a_codes", align_bytes=64)
-        a_plane = pool.tile([P, R], U8, name="a_plane", align_bytes=64)
-        nc.vector.quantize_mx(out=a_codes[:].bitcast(FP8X4), scales=a_plane[:], in_=woven_a[:].rearrange("p t m i -> p (t m i)"))
+        planes = look_up("b1", list_b, step_b, 1, picked_tile("picked_b1", 4, "a0_2"))
 
-        planes = look_up("b0", list_b, step_b, 0, picked_tile("picked_b0", 4, "b0"))
-        weave(nc.scalar.copy, woven_b[0][:], planes, 0, PACK)
-        planes = look_up("b1", list_b, step_b, 1, picked_tile("picked_b1_01", 2, "b1_01") + picked_tile("picked_b1_23", 2, "woven_a"))
+        def quantize(name, values):
+            width = values.shape[1] // PACK
+            codes = pool.tile([P, width], I32, name=name + "_codes", align_bytes=64)
+            plane = pool.tile([P, width], U8, name=name + "_plane", align_bytes=64)
+            nc.vector.quantize_mx(out=codes[:].bitcast(FP8X4), scales=plane[:], in_=values)
+            return codes, plane
+
+        a_pairs = [quantize("a%d" % u, woven_a[:, 2 * u : 2 * u + 2, :, :].rearrange("p t m i -> p (t m i)")) for u in range(2)]
 
         b_codes = [pool.tile([P, P], I32, name="b_codes%d" % t, align_bytes=64) for t in range(PACK)]
         b_plane = [pool.tile([P, P], U8, name="b_plane%d" % t, align_bytes=64) for t in range(PACK)]
 
-        def quantize_b(t, half):
-            cols = slice(half * HALF_M, (half + 1) * HALF_M)
+        def quantize_b(t, m0, m1):
             nc.vector.quantize_mx(
-                out=b_codes[t][:, cols].bitcast(FP8X4),
-                scales=b_plane[t][:, cols],
-                in_=woven_b[half][:, t, :, :].rearrange("p m i -> p (m i)"),
+                out=b_codes[t][:, m0:m1].bitcast(FP8X4),
+                scales=b_plane[t][:, m0:m1],
+                in_=woven_b[:, t, m0:m1, :].rearrange("p m i -> p (m i)"),
             )
 
-        for t in range(PACK):
-            quantize_b(t, 0)
-        weave(nc.scalar.copy, woven_b[1][:], planes, VECTOR_T, PACK)
-        weave(nc.vector.tensor_copy, woven_b[1][:], planes, 0, VECTOR_T)
+        weave(nc.scalar.copy, woven_b[:, :, HALF_M:, :], planes, VECTOR_T, PACK)
+        weave(nc.vector.tensor_copy, woven_b[:, :, HALF_M:, :], planes, 0, VECTOR_T)
 
-        def first_product(acc, codes, plane):
+        def first_product(acc, codes, plane, cols):
             nc.tensor.matmul_mx(
                 out=acc,
                 lhsT=codes.bitcast(FP8X4),
                 lhsT_scale=plane,
-                rhs=xg_words[:].bitcast(FP4X4),
-                rhs_scale=xg_scales[:],
+                rhs=xg_words[:, cols].bitcast(FP4X4),
+                rhs_scale=xg_scales[:, cols],
                 start=True,
                 stop=True,
             )
 
-        a_kept = []
+        def in_order(c, pair):
+            return pair if c == 0 else pair.rearrange("p e j -> p j e")
+
+        def laid(c, flat):
+            return flat.rearrange("p (e j) -> p e j", e=2) if c == 0 else flat.rearrange("p (j e) -> p j e", e=2)
+
+        j_cols = [slice(c * J_PART, (c + 1) * J_PART) for c in range(J_PARTS)]
+        a_banks = []
         for u in range(2):
-            a_bank = psum.tile([P, 2, J], F32, name="a_bank%d" % u)
+            a_bank = psum.tile([P, 2, J], F32, name="a_bank%d" % u, tag="bank%d" % u)
             for e in range(2):
-                cols = slice((2 * u + e) * P, (2 * u + e + 1) * P)
-                first_product(a_bank[:, e, :], a_codes[:, cols], a_plane[:, cols])
-            kept = pool.tile([P, J, 2], F32, name="a_kept%d" % u)
-            nc.scalar.copy(kept[:], a_bank[:].rearrange("p e j -> p j e"))
-            a_kept.append(kept)
-
-        b_banks = []
-        for u in range(2):
-            b_bank = psum.tile([P, 2, J], F32, name="b_bank%d" % u)
-            for e in range(2):
-                t = 2 * u + e
-                quantize_b(t, 1)
-                first_product(b_bank[:, e, :], b_codes[t][:], b_plane[t][:])
-            b_banks.append(b_bank)
-
-        larger = pool.tile([P, 2, J, 2], F32, name="larger")
-        for u in range(2):
-            nc.vector.tensor_tensor(larger[:, u, :, :], b_banks[u][:].rearrange("p e j -> p j e"), a_kept[u][:], MAX)
-
-        hids = []
+                codes, plane = a_pairs[u]
+                first_product(a_bank[:, e, :], codes[:, e * P : (e + 1) * P], plane[:, e * P : (e + 1) * P], slice(0, J))
+            a_banks.append(a_bank)
+        a_kept = pool.tile([P, J_PARTS, 2, 2 * J_PART], F32, name="a_kept", tag="a0_2", align_bytes=64)
         for c in range(J_PARTS):
-            hid = pool.tile([P, J_PART, 2, 2], BF16, name="hid%d" % c, align_bytes=64)
-            nc.vector.tensor_tensor(
-                hid[:],
-                larger[:, :, c * J_PART : (c + 1) * J_PART, :].rearrange("p u j e -> p j u e"),
-                weight_r[:].rearrange("p (u e) -> p u e", u=2).unsqueeze(1).to_broadcast([P, J_PART, 2, 2]),
-                MULT,
+            for u in range(2):
+                nc.scalar.copy(laid(c, a_kept[:, c, u, :]), in_order(c, a_banks[u][:, :, j_cols[c]]))
+
+        for t in range(PACK):
+            quantize_b(t, 0, P)
+        larger = pool.tile([P, J_PARTS, 2, 2 * J_PART], F32, name="larger")
+        for c in range(J_PARTS):
+            for u in range(2):
+                b_bank = psum.tile([P, 2, J_PART], F32, name="b_bank%d%d" % (c, u), tag="bank%d" % (u + 2 * (1 - c)))
+                for e in range(2):
+                    first_product(b_bank[:, e, :], b_codes[2 * u + e][:], b_plane[2 * u + e][:], j_cols[c])
+                nc.vector.tensor_tensor(laid(c, larger[:, c, u, :]), in_order(c, b_bank[:]), laid(c, a_kept[:, c, u, :]), MAX)
+
+        hid = pool.tile([P, J, PACK], BF16, name="hid", align_bytes=64)
+        hid_planes = pool.tile([P, PACK, J_PART], BF16, name="hid_planes")
+        for t in range(PACK):
+            nc.scalar.activation(
+                out=hid_planes[:, t, :], in_=laid(0, larger[:, 0, t // 2, :])[:, t % 2, :], func=COPY, scale=weight_r[:, t : t + 1]
             )
-            hids.append(hid)
+        nc.scalar.copy(
+            hid[:, j_cols[0], :].rearrange("p (c i) t -> p c t i", i=4),
+            hid_planes[:].rearrange("p t (c i) -> p c t i", i=4),
+        )
+        nc.vector.tensor_tensor(
+            hid[:, j_cols[1], :].rearrange("p j (u e) -> p j u e", u=2),
+            larger[:, 1, :, :].rearrange("p u (j e) -> p j u e", e=2),
+            weight_r[:].rearrange("p (u e) -> p u e", u=2).unsqueeze(1).to_broadcast([P, J_PART, 2, 2]),
+            MULT,
+        )
 
         out_rows = out.rearrange("(g p) j -> p g j", p=P)
         for c in range(J_PARTS):
+            cols = slice(c * J_PART, (c + 1) * J_PART)
             h_codes = pool.tile([P, J_PART], I32, name="h_codes%d" % c, align_bytes=64)
             h_plane = pool.tile([P, J_PART], U8, name="h_plane%d" % c, align_bytes=64)
-            nc.vector.quantize_mx(out=h_codes[:].bitcast(FP8X4), scales=h_plane[:], in_=hids[c][:].rearrange("p j u e -> p (j u e)"))
-            o_bank = psum.tile([P, N // P, J_PART], F32, name="o_bank%d" % c)
-            for g in range(N // P):
+            nc.vector.quantize_mx(out=h_codes[:].bitcast(FP8X4), scales=h_plane[:], in_=hid[:, cols, :].rearrange("p j t -> p (j t)"))
+
+            for g, copy in enumerate((nc.vector.tensor_copy, nc.scalar.copy)):
+                o_bank = psum.tile([P, J_PART], F32, name="o_bank%d%d" % (c, g))
                 nc.tensor.matmul_mx(
-                    out=o_bank[:, g, :],
+                    out=o_bank[:],
                     lhsT=wb_codes[:, g * P : (g + 1) * P].bitcast(FP8X4),
                     lhsT_scale=wb_plane[:, g * P : (g + 1) * P],
                     rhs=h_codes[:].bitcast(FP8X4),
@@ -180,9 +198,7 @@ def tile_list_rivalcolumns_kernel(tc, xt_words, xt_scales, ca, sa, sb, sr, wb_wo
                     start=True,
                     stop=True,
                 )
-            result = pool.tile([P, N // P, J_PART], F32, name="result%d" % c)
-            if c == 0:
-                nc.scalar.copy(result[:], o_bank[:])
-            else:
-                nc.vector.tensor_copy(result[:], o_bank[:])
-            nc.sync.dma_start(out_rows[:, :, c * J_PART : (c + 1) * J_PART], result[:])
+                result = pool.tile([P, J_PART], F32, name="result%d%d" % (c, g))
+                copy(result[:], o_bank[:])
+                queue = nc.scalar if (c, g) == (J_PARTS - 1, 1) else nc.sync
+                queue.dma_start(out_rows[:, g, cols], result[:])

from contextlib import ExitStack

import concourse.mybir as mybir

K, T, V, J, R, N = 512, 1024, 2048, 256, 512, 256
FLOPS = 2 * (2 * K * R * J + R * N * J)

F32 = mybir.dt.float32
BF16 = mybir.dt.bfloat16
I32 = mybir.dt.int32
U16 = mybir.dt.uint16
U8 = mybir.dt.uint8
FP8 = mybir.dt.float8_e4m3fn
FP8X4 = mybir.dt.float8_e4m3fn_x4
FP4X4 = mybir.dt.float4_e2m1fn_x4
COPY = mybir.ActivationFunctionType.Copy
MAX = mybir.AluOpType.max
MULT = mybir.AluOpType.mult

P = 128
PACK = 4
HALVES = 2
HALF = R // HALVES
HALF_M = HALF // PACK
J_PARTS = 2
J_PART = J // J_PARTS
VECTOR_T = 2


def tile_list_rivalcolumns_kernel(tc, xt_words, xt_scales, ca, sa, sb, sr, wb_words, wb_scales, offs, offs2, offs3, out):
    nc = tc.nc
    with ExitStack() as ctx:
        pool = ctx.enter_context(tc.tile_pool(name="pool", bufs=1))
        psum = ctx.enter_context(tc.psum_pool(name="psum", bufs=1))

        list_a = pool.tile([P, R // 16], U16, name="list_a")
        list_b = pool.tile([P, R // 16], U16, name="list_b")
        list_x = pool.tile([P, J // 16], U16, name="list_x")
        table = [pool.tile([P, V], U8, name="table%d" % i) for i in range(PACK)]
        step_a = pool.tile([P, PACK], F32, name="step_a")
        step_b = pool.tile([P, PACK], F32, name="step_b")
        weight_r = pool.tile([P, PACK], F32, name="weight_r")
        x_words = pool.tile([P, T], U16, name="x_words")
        x_scales = pool.tile([P, T], U8, name="x_scales")
        wb_codes = pool.tile([P, N], I32, name="wb_codes", align_bytes=64)
        wb_plane = pool.tile([P, N], U8, name="wb_plane", align_bytes=64)

        nc.vector.memset(x_scales[:].bitcast(I32), 0)
        nc.vector.memset(wb_plane[:].bitcast(I32), 0)

        ca_rows = ca.rearrange("(p i) v -> p i v", i=PACK)
        nc.sync.dma_start(table[0][:], ca_rows[:, 0, :])
        nc.sync.dma_start(list_a[:], offs)
        nc.scalar.dma_start(step_a[:], sa.rearrange("(p i) o -> p (i o)", i=PACK))
        for i in range(1, PACK):
            nc.sync.dma_start(table[i][:], ca_rows[:, i, :])
        nc.sync.dma_start(list_b[:], offs2)
        nc.sync.dma_start(step_b[:], sb.rearrange("(p i) o -> p (i o)", i=PACK))
        nc.sync.dma_start(list_x[:], offs3)
        nc.sync.dma_start(x_words[:].bitcast(I32), xt_words[0].bitcast(I32))
        for q in range(4):
            nc.sync.dma_start(x_scales[32 * q : 32 * q + 4, :].bitcast(I32), xt_scales[0, 4 * q : 4 * q + 4, :].bitcast(I32))
        nc.sync.dma_start(weight_r[:], sr.rearrange("(p t) o -> p (t o)", t=PACK))
        nc.sync.dma_start(wb_codes[:], wb_words[0].rearrange("p n t -> p (n t)").bitcast(I32))
        for q in range(4):
            nc.sync.dma_start(wb_plane[32 * q : 32 * q + 4, :].bitcast(I32), wb_scales[0, 4 * q : 4 * q + 4, :].bitcast(I32))

        def look_up(name, offsets, step, half, picked):
            planes = pool.tile([P, PACK, HALF], BF16, name="planes_" + name, tag="planes")
            cols = HALF // 16
            for i in range(PACK):
                nc.vector.tensor_copy(picked[i], table[i][:].indirect(offsets[:, half * cols : (half + 1) * cols]))
                nc.scalar.activation(out=planes[:, i, :], in_=picked[i].bitcast(FP8), func=COPY, scale=step[:, i : i + 1])
            return planes

        def picked_tile(name, count, tag):
            picked = pool.tile([P, count, HALF], U8, name=name, tag=tag, align_bytes=64)
            return [picked[:, i, :] for i in range(count)]

        def weave(copy, woven, planes, t0, t1):
            copy(
                woven[:, t0:t1, :, :].rearrange("p t m i -> p m i t"),
                planes[:].rearrange("p i (m t) -> p m i t", t=PACK)[:, :, :, t0:t1],
            )

        woven_a = pool.tile([P, PACK, P, PACK], BF16, name="woven_a", align_bytes=64)
        picked = picked_tile("picked_a0_01", 2, "a0_01") + picked_tile("picked_a0_2", 1, "a0_2") + picked_tile("picked_a0_3", 1, "a0_3")
        planes = look_up("a0", list_a, step_a, 0, picked)
        weave(nc.scalar.copy, woven_a[:, :, :HALF_M, :], planes, 0, PACK)
        planes = look_up("a1", list_a, step_a, 1, picked_tile("picked_a1", 4, "a0_2"))
        weave(nc.scalar.copy, woven_a[:, :, HALF_M:, :], planes, 0, PACK)

        woven_b = pool.tile([P, PACK, P, PACK], BF16, name="woven_b", align_bytes=64)
        planes = look_up("b0", list_b, step_b, 0, picked_tile("picked_b0", 4, "a0_3"))
        weave(nc.scalar.copy, woven_b[:, :, :HALF_M, :], planes, 0, PACK)

        xg_words = pool.tile([P, J], U16, name="xg_words", align_bytes=64)
        xg_scales = pool.tile([P, J], U8, name="xg_scales", align_bytes=64)
        nc.vector.tensor_copy(xg_words[:], x_words[:].indirect(list_x[:]))
        nc.vector.tensor_copy(xg_scales[:], x_scales[:].indirect(list_x[:]))

        planes = look_up("b1", list_b, step_b, 1, picked_tile("picked_b1", 4, "a0_2"))

        def quantize(name, values):
            width = values.shape[1] // PACK
            codes = pool.tile([P, width], I32, name=name + "_codes", align_bytes=64)
            plane = pool.tile([P, width], U8, name=name + "_plane", align_bytes=64)
            nc.vector.quantize_mx(out=codes[:].bitcast(FP8X4), scales=plane[:], in_=values)
            return codes, plane

        a_pairs = [quantize("a%d" % u, woven_a[:, 2 * u : 2 * u + 2, :, :].rearrange("p t m i -> p (t m i)")) for u in range(2)]

        b_codes = [pool.tile([P, P], I32, name="b_codes%d" % t, align_bytes=64) for t in range(PACK)]
        b_plane = [pool.tile([P, P], U8, name="b_plane%d" % t, align_bytes=64) for t in range(PACK)]

        def quantize_b(t, m0, m1):
            nc.vector.quantize_mx(
                out=b_codes[t][:, m0:m1].bitcast(FP8X4),
                scales=b_plane[t][:, m0:m1],
                in_=woven_b[:, t, m0:m1, :].rearrange("p m i -> p (m i)"),
            )

        weave(nc.scalar.copy, woven_b[:, :, HALF_M:, :], planes, VECTOR_T, PACK)
        weave(nc.vector.tensor_copy, woven_b[:, :, HALF_M:, :], planes, 0, VECTOR_T)

        def first_product(acc, codes, plane, cols):
            nc.tensor.matmul_mx(
                out=acc,
                lhsT=codes.bitcast(FP8X4),
                lhsT_scale=plane,
                rhs=xg_words[:, cols].bitcast(FP4X4),
                rhs_scale=xg_scales[:, cols],
                start=True,
                stop=True,
            )

        def in_order(c, pair):
            return pair if c == 0 else pair.rearrange("p e j -> p j e")

        def laid(c, flat):
            return flat.rearrange("p (e j) -> p e j", e=2) if c == 0 else flat.rearrange("p (j e) -> p j e", e=2)

        j_cols = [slice(c * J_PART, (c + 1) * J_PART) for c in range(J_PARTS)]
        a_banks = []
        for u in range(2):
            a_bank = psum.tile([P, 2, J], F32, name="a_bank%d" % u, tag="bank%d" % u)
            for e in range(2):
                codes, plane = a_pairs[u]
                first_product(a_bank[:, e, :], codes[:, e * P : (e + 1) * P], plane[:, e * P : (e + 1) * P], slice(0, J))
            a_banks.append(a_bank)
        a_kept = pool.tile([P, J_PARTS, 2, 2 * J_PART], F32, name="a_kept", tag="a0_2", align_bytes=64)
        for c in range(J_PARTS):
            for u in range(2):
                nc.scalar.copy(laid(c, a_kept[:, c, u, :]), in_order(c, a_banks[u][:, :, j_cols[c]]))

        for t in range(PACK):
            quantize_b(t, 0, P)
        larger = pool.tile([P, J_PARTS, 2, 2 * J_PART], F32, name="larger")
        for c in range(J_PARTS):
            for u in range(2):
                b_bank = psum.tile([P, 2, J_PART], F32, name="b_bank%d%d" % (c, u), tag="bank%d" % (u + 2 * (1 - c)))
                for e in range(2):
                    first_product(b_bank[:, e, :], b_codes[2 * u + e][:], b_plane[2 * u + e][:], j_cols[c])
                nc.vector.tensor_tensor(laid(c, larger[:, c, u, :]), in_order(c, b_bank[:]), laid(c, a_kept[:, c, u, :]), MAX)

        hid = pool.tile([P, J, PACK], BF16, name="hid", align_bytes=64)
        hid_planes = pool.tile([P, PACK, J_PART], BF16, name="hid_planes")
        for t in range(PACK):
            nc.scalar.activation(
                out=hid_planes[:, t, :], in_=laid(0, larger[:, 0, t // 2, :])[:, t % 2, :], func=COPY, scale=weight_r[:, t : t + 1]
            )
        nc.scalar.copy(
            hid[:, j_cols[0], :].rearrange("p (c i) t -> p c t i", i=4),
            hid_planes[:].rearrange("p t (c i) -> p c t i", i=4),
        )
        nc.vector.tensor_tensor(
            hid[:, j_cols[1], :].rearrange("p j (u e) -> p j u e", u=2),
            larger[:, 1, :, :].rearrange("p u (j e) -> p j u e", e=2),
            weight_r[:].rearrange("p (u e) -> p u e", u=2).unsqueeze(1).to_broadcast([P, J_PART, 2, 2]),
            MULT,
        )

        out_rows = out.rearrange("(g p) j -> p g j", p=P)
        for c in range(J_PARTS):
            cols = slice(c * J_PART, (c + 1) * J_PART)
            h_codes = pool.tile([P, J_PART], I32, name="h_codes%d" % c, align_bytes=64)
            h_plane = pool.tile([P, J_PART], U8, name="h_plane%d" % c, align_bytes=64)
            nc.vector.quantize_mx(out=h_codes[:].bitcast(FP8X4), scales=h_plane[:], in_=hid[:, cols, :].rearrange("p j t -> p (j t)"))

            for g, copy in enumerate((nc.vector.tensor_copy, nc.scalar.copy)):
                o_bank = psum.tile([P, J_PART], F32, name="o_bank%d%d" % (c, g))
                nc.tensor.matmul_mx(
                    out=o_bank[:],
                    lhsT=wb_codes[:, g * P : (g + 1) * P].bitcast(FP8X4),
                    lhsT_scale=wb_plane[:, g * P : (g + 1) * P],
                    rhs=h_codes[:].bitcast(FP8X4),
                    rhs_scale=h_plane[:],
                    start=True,
                    stop=True,
                )
                result = pool.tile([P, J_PART], F32, name="result%d%d" % (c, g))
                copy(result[:], o_bank[:])
                queue = nc.scalar if (c, g) == (J_PARTS - 1, 1) else nc.sync
                queue.dma_start(out_rows[:, g, cols], result[:])
